import numpy as np, ml_dtypes
CORES = [3,5,19,21,35,37,51,53,67,69]
N = 10
F = 128
BETA, LR = 0.75, 0.5
def setup_inputs(rng):
    return {"gr": rng.standard_normal((N, 128, N * F), dtype=np.float32).astype(ml_dtypes.bfloat16), "m": rng.standard_normal((N, 128, F), dtype=np.float32).astype(ml_dtypes.bfloat16), "w": rng.standard_normal((N, 128, F), dtype=np.float32).astype(ml_dtypes.bfloat16)}
def setup_inputs_big(rng):
    d = setup_inputs(rng)
    for k in ("gr", "m", "w"): d[k] = (d[k].astype(np.float32) * 1048576.0).astype(d[k].dtype)
    return d
def setup_inputs_small(rng):
    d = setup_inputs(rng)
    for k in ("gr", "m", "w"): d[k] = (d[k].astype(np.float32) * (1 / 1048576.0)).astype(d[k].dtype)
    return d
def setup_inputs_apart(rng):
    d = setup_inputs(rng)
    f = (10.0 ** rng.permutation(np.linspace(-1.5, 1.5, N))).astype(np.float32).reshape(N, 1, 1)
    for k in ("gr", "m", "w"): d[k] = (d[k].astype(np.float32) * f).astype(d[k].dtype)
    return d
def reference(gr, m, w):
    GR, M, W = gr.astype(np.float64), m.astype(np.float64), w.astype(np.float64)
    s = GR.sum(axis=0)
    m2 = np.stack([BETA * M[r] + s[:, F * r:F * r + F] for r in range(N)])
    w2 = np.concatenate([W[r] - LR * m2[r] for r in range(N)], axis=1)
    return {"y": np.broadcast_to(w2.astype(ml_dtypes.bfloat16), (N, 128, N * F)), "mo": m2.astype(ml_dtypes.bfloat16)}

@@ -1,0 +1,164 @@
+from concourse.bass import DstId, RemoteDMATransfer
+from concourse.mybir import AluOpType
+
+N = 10
+F = 128
+W = N * F
+
+SCRATCH = {
+    "gsb": ("sbuf", [128, W], "bfloat16"),
+    "csb": ("sbuf", [128, W], "bfloat16"),
+    "msb": ("sbuf", [128, F], "bfloat16"),
+    "wsb": ("sbuf", [128, F], "bfloat16"),
+    "ysb": ("sbuf", [128, F], "bfloat16"),
+    "dsb": ("sbuf", [128, F], "float32"),
+    "mosb": ("sbuf", [128, F], "bfloat16"),
+    "khalf": ("psum", [128, 512], "float32"),
+    "k375": ("psum", [128, F], "float32"),
+    "tps": ("psum", [128, F], "float32"),
+    "ups": ("psum", [128, F], "float32"),
+    "G": ("dram", [W, F], "bfloat16"),
+    "Lnd": ("dram", [W, F], "bfloat16"),
+    "Y": ("dram", [W, F], "bfloat16"),
+}
+SEMAPHORES = ["ld_g", "ld_mw", "vs", "st_g", "garr", "yarr", "ls", "ldy", "vt", "fin"]
+
+
+def _engines(mask):
+    return [e for e in range(mask.bit_length()) if (mask >> e) & 1]
+
+
+def _bits(engs):
+    m = 0
+    for e in engs:
+        m |= 1 << e
+    return m
+
+
+def _spread(engs, k):
+    return [engs[(i * len(engs)) // k] for i in range(k)]
+
+
+def _keepers(cores, topo):
+    out = []
+    for c in cores:
+        for k in range(topo.CORES_PER_CHIP * topo.CHIPS):
+            if k in cores or k in out:
+                continue
+            if topo.chip(k) != topo.chip(c) or topo.die(k) != topo.die(c):
+                continue
+            if all(topo.may_write(k, r) and topo.may_write(r, k) for r in cores):
+                out.append(k)
+                break
+    return out
+
+
+def _dst(topo, c):
+    rid, pid, _se = topo.addr(c)
+    return DstId(rid=rid, pnc=pid)
+
+
+def _keeper_masks(k, cores, topo):
+    off = [r for r in cores if topo.chip(r) != topo.chip(k)]
+    on = [r for r in cores if topo.chip(r) == topo.chip(k)]
+    m_off = topo.mask(k, off[0])
+    for r in off:
+        m_off &= topo.mask(k, r)
+    m_on = topo.mask(k, on[0])
+    for r in on:
+        m_on &= topo.mask(k, r)
+    m_on = _bits(_spread(_engines(m_on & ~m_off), 2))
+    return off, on, m_off, m_on
+
+
+def _piece(t, j):
+    return t[128 * j:128 * j + 128, :]
+
+
+def _keeper(g, core, T, topo, cores, j):
+    S = T.sem
+    off, on, m_off, m_on = _keeper_masks(core, cores, topo)
+    g.wait_ge(S.garr, N)
+    srcs = [_piece(T.Lnd, s) for s in range(N)]
+    tr = [
+        RemoteDMATransfer(dst_ids=[_dst(topo, r) for r in off], dma_engine_mask=m_off, remote_sem=S.yarr,
+                          srcs=srcs, dsts=[_piece(T.Y, j) for _ in off], alu_op=1),
+        RemoteDMATransfer(dst_ids=[_dst(topo, r) for r in on], dma_engine_mask=m_on, remote_sem=S.yarr,
+                          srcs=srcs, dsts=[_piece(T.Y, j) for _ in on], alu_op=1),
+    ]
+    g.remote_dma_fused(tr, local_sem=S.ls)
+    g.wait_ge(S.ls, len(_engines(m_off)) + len(_engines(m_on)))
+
+
+def _rank(g, core, T, topo, cores, keepers, rank):
+    S = T.sem
+    v = g.vector
+    b0 = F * rank
+    g.sync.dma_start(T.gsb[:], T.gr[:]).then_inc(S.ld_g, 16)
+    g.scalar.dma_start(T.msb[:], T.m[:]).then_inc(S.ld_mw, 16)
+    g.scalar.dma_start(T.wsb[:], T.w[:]).then_inc(S.ld_mw, 16)
+    v.memset(T.khalf[:], -0.5).then_inc(S.vs, 1)
+    v.memset(T.k375[:], -0.375).then_inc(S.vs, 1)
+    n = 2
+    v.wait_ge(S.vs, n)
+    v.wait_ge(S.ld_mw, 32)
+    v.tensor_tensor(T.tps[:], T.msb[:], T.k375[:], AluOpType.mult).then_inc(S.vs, 1)
+    n += 1
+    v.wait_ge(S.vs, n)
+    v.tensor_tensor(T.ups[:], T.wsb[:], T.tps[:], AluOpType.add).then_inc(S.vs, 1)
+    n += 1
+    v.wait_ge(S.vs, n)
+    v.wait_ge(S.ld_g, 16)
+    parts = [(a, min(a + 512, W)) for a in range(0, W, 512)]
+    parts.sort(key=lambda ab: 0 if ab[0] <= b0 < ab[1] else 1)
+    for i, (a, b) in enumerate(parts):
+        v.tensor_tensor(T.csb[:, a:b], T.gsb[:, a:b], T.khalf[:, 0:b - a], AluOpType.mult).then_inc(S.vs, 1)
+        n += 1
+        if i == 0:
+            v.wait_ge(S.vs, n)
+            v.tensor_tensor(T.csb[:, b0:b0 + F], T.csb[:, b0:b0 + F], T.ups[:], AluOpType.add).then_inc(S.vs, 1)
+            n += 1
+    g.sync.wait_ge(S.vs, n)
+    g.sync.dma_start(T.G[:], T.csb[:]).then_inc(S.st_g, 16)
+    g.wait_ge(S.st_g, 16)
+    off = [j for j in range(N) if topo.chip(keepers[j]) != topo.chip(core)]
+    on = [j for j in range(N) if topo.chip(keepers[j]) == topo.chip(core)]
+    tr = []
+    used = 0
+    for j in off:
+        e = _engines(topo.mask(core, keepers[j]) & ~used)[0]
+        used |= 1 << e
+        tr.append((j, e))
+    free = topo.mask(core, keepers[on[0]]) & ~used
+    for j, e in zip(on, _spread(_engines(free), len(on))):
+        tr.append((j, e))
+    g.remote_dma_fused(
+        [RemoteDMATransfer(dst_ids=[_dst(topo, keepers[j])], dma_engine_mask=1 << e, remote_sem=S.garr,
+                           src=_piece(T.G, j), dst=_piece(T.Lnd, rank)) for j, e in tr],
+        local_sem=S.ls)
+    total = 0
+    for k in keepers:
+        _o, _n, m_off, m_on = _keeper_masks(k, cores, topo)
+        total += len(_engines(m_on if topo.chip(k) == topo.chip(core) else m_off))
+    g.scalar.wait_ge(S.yarr, total)
+    g.scalar.dma_start(T.ysb[:], T.Y[rank::N, :]).then_inc(S.ldy, 16)
+    g.sync.wait_ge(S.yarr, total)
+    g.sync.dma_start(T.y[:], T.Y[:]).then_inc(S.fin, 16)
+    v.wait_ge(S.ldy, 16)
+    v.tensor_tensor(T.dsb[:], T.wsb[:], T.ysb[:], AluOpType.subtract).then_inc(S.vt, 1)
+    v.wait_ge(S.vt, 1)
+    v.tensor_tensor(T.mosb[:], T.dsb[:], T.dsb[:], AluOpType.add).then_inc(S.vt, 1)
+    g.scalar.wait_ge(S.vt, 2)
+    g.scalar.dma_start(T.mo[:], T.mosb[:]).then_inc(S.fin, 16)
+    g.wait_ge(S.ls, len(tr))
+    g.wait_ge(S.fin, 32)
+
+
+def rank_program(g, core, T, topo):
+    cores = list(T.cores)
+    keepers = _keepers(cores, topo)
+    rank = T.rank_of(core)
+    if rank is not None:
+        _rank(g, core, T, topo, cores, keepers, rank)
+    elif core in keepers:
+        _keeper(g, core, T, topo, cores, keepers.index(core))

@@ -7,50 +7,29 @@ W = N * F
 
 SCRATCH = {
     "gsb": ("sbuf", [128, W], "bfloat16"),
-    "csb": ("sbuf", [128, W], "bfloat16"),
+    "land": ("sbuf", [128, W], "bfloat16"),
+    "ysb": ("sbuf", [128, W], "bfloat16"),
     "msb": ("sbuf", [128, F], "bfloat16"),
     "wsb": ("sbuf", [128, F], "bfloat16"),
-    "ysb": ("sbuf", [128, F], "bfloat16"),
-    "dsb": ("sbuf", [128, F], "float32"),
+    "m75": ("sbuf", [128, F], "bfloat16"),
+    "usb": ("sbuf", [128, F], "bfloat16"),
     "mosb": ("sbuf", [128, F], "bfloat16"),
-    "khalf": ("psum", [128, 512], "float32"),
-    "k375": ("psum", [128, F], "float32"),
-    "tps": ("psum", [128, F], "float32"),
-    "ups": ("psum", [128, F], "float32"),
-    "G": ("dram", [W, F], "bfloat16"),
-    "Lnd": ("dram", [W, F], "bfloat16"),
-    "Y": ("dram", [W, F], "bfloat16"),
+    "z1": ("sbuf", [128, F + 1], "bfloat16"),
+    "z2": ("sbuf", [128, F + 1], "bfloat16"),
+    "eye": ("sbuf", [128, F], "bfloat16"),
+    "hlf": ("sbuf", [128, F], "bfloat16"),
+    "D": ("dram", [2, F + 1, F], "bfloat16"),
+    "k75": ("psum", [128, 512], "float32"),
+    "tps": ("psum", [128, 512], "float32"),
+    "P": ("psum", [128, 512], "float32"),
+    "Q": ("psum", [128, 512], "float32"),
 }
-SEMAPHORES = ["ld_g", "ld_mw", "vs", "st_g", "garr", "yarr", "ls", "ldy", "vt", "fin"]
+SEMAPHORES = ["ld_g", "ld_mw", "vz", "vs", "dz", "de", "qd", "pd", "wd", "md", "yarr", "ls", "fin"] + \
+             ["a%d" % s for s in range(N)]
 
 
 def _engines(mask):
     return [e for e in range(mask.bit_length()) if (mask >> e) & 1]
-
-
-def _bits(engs):
-    m = 0
-    for e in engs:
-        m |= 1 << e
-    return m
-
-
-def _spread(engs, k):
-    return [engs[(i * len(engs)) // k] for i in range(k)]
-
-
-def _keepers(cores, topo):
-    out = []
-    for c in cores:
-        for k in range(topo.CORES_PER_CHIP * topo.CHIPS):
-            if k in cores or k in out:
-                continue
-            if topo.chip(k) != topo.chip(c) or topo.die(k) != topo.die(c):
-                continue
-            if all(topo.may_write(k, r) and topo.may_write(r, k) for r in cores):
-                out.append(k)
-                break
-    return out
 
 
 def _dst(topo, c):
@@ -58,107 +37,81 @@ def _dst(topo, c):
     return DstId(rid=rid, pnc=pid)
 
 
-def _keeper_masks(k, cores, topo):
-    off = [r for r in cores if topo.chip(r) != topo.chip(k)]
-    on = [r for r in cores if topo.chip(r) == topo.chip(k)]
-    m_off = topo.mask(k, off[0])
-    for r in off:
-        m_off &= topo.mask(k, r)
-    m_on = topo.mask(k, on[0])
-    for r in on:
-        m_on &= topo.mask(k, r)
-    m_on = _bits(_spread(_engines(m_on & ~m_off), 2))
-    return off, on, m_off, m_on
-
-
-def _piece(t, j):
-    return t[128 * j:128 * j + 128, :]
-
-
-def _keeper(g, core, T, topo, cores, j):
-    S = T.sem
-    off, on, m_off, m_on = _keeper_masks(core, cores, topo)
-    g.wait_ge(S.garr, N)
-    srcs = [_piece(T.Lnd, s) for s in range(N)]
-    tr = [
-        RemoteDMATransfer(dst_ids=[_dst(topo, r) for r in off], dma_engine_mask=m_off, remote_sem=S.yarr,
-                          srcs=srcs, dsts=[_piece(T.Y, j) for _ in off], alu_op=1),
-        RemoteDMATransfer(dst_ids=[_dst(topo, r) for r in on], dma_engine_mask=m_on, remote_sem=S.yarr,
-                          srcs=srcs, dsts=[_piece(T.Y, j) for _ in on], alu_op=1),
-    ]
-    g.remote_dma_fused(tr, local_sem=S.ls)
-    g.wait_ge(S.ls, len(_engines(m_off)) + len(_engines(m_on)))
-
-
-def _rank(g, core, T, topo, cores, keepers, rank):
+def rank_program(g, core, T, topo):
+    rank = T.rank_of(core)
+    if rank is None:
+        return
+    cores = list(T.cores)
     S = T.sem
     v = g.vector
-    b0 = F * rank
+    te = g.tensor
+    own = slice(F * rank, F * rank + F)
     g.sync.dma_start(T.gsb[:], T.gr[:]).then_inc(S.ld_g, 16)
     g.scalar.dma_start(T.msb[:], T.m[:]).then_inc(S.ld_mw, 16)
     g.scalar.dma_start(T.wsb[:], T.w[:]).then_inc(S.ld_mw, 16)
-    v.memset(T.khalf[:], -0.5).then_inc(S.vs, 1)
-    v.memset(T.k375[:], -0.375).then_inc(S.vs, 1)
-    n = 2
-    v.wait_ge(S.vs, n)
+    v.memset(T.z1[:], 0.0).then_inc(S.vz, 1)
+    v.memset(T.z2[:], 0.0).then_inc(S.vz, 1)
+    v.wait_ge(S.vz, 2)
+    v.memset(T.z1[:, 0:1], 1.0).then_inc(S.vz, 1)
+    v.memset(T.z2[:, 0:1], -0.5).then_inc(S.vz, 1)
+    g.scalar.wait_ge(S.vz, 4)
+    g.scalar.dma_start(T.D[0], T.z1[:]).then_inc(S.dz, 16)
+    g.scalar.dma_start(T.D[1], T.z2[:]).then_inc(S.dz, 16)
+    g.scalar.wait_ge(S.dz, 32)
+    g.scalar.dma_start(T.eye[:], T.D[0, 0:F, :]).then_inc(S.de, 16)
+    g.scalar.dma_start(T.hlf[:], T.D[1, 0:F, :]).then_inc(S.de, 16)
+    v.memset(T.k75[:, 0:F], 0.75).then_inc(S.vs, 1)
+    v.memset(T.k75[:, F:2 * F], -0.375).then_inc(S.vs, 1)
+    v.wait_ge(S.vs, 2)
     v.wait_ge(S.ld_mw, 32)
-    v.tensor_tensor(T.tps[:], T.msb[:], T.k375[:], AluOpType.mult).then_inc(S.vs, 1)
-    n += 1
-    v.wait_ge(S.vs, n)
-    v.tensor_tensor(T.ups[:], T.wsb[:], T.tps[:], AluOpType.add).then_inc(S.vs, 1)
-    n += 1
-    v.wait_ge(S.vs, n)
-    v.wait_ge(S.ld_g, 16)
-    parts = [(a, min(a + 512, W)) for a in range(0, W, 512)]
-    parts.sort(key=lambda ab: 0 if ab[0] <= b0 < ab[1] else 1)
-    for i, (a, b) in enumerate(parts):
-        v.tensor_tensor(T.csb[:, a:b], T.gsb[:, a:b], T.khalf[:, 0:b - a], AluOpType.mult).then_inc(S.vs, 1)
-        n += 1
-        if i == 0:
-            v.wait_ge(S.vs, n)
-            v.tensor_tensor(T.csb[:, b0:b0 + F], T.csb[:, b0:b0 + F], T.ups[:], AluOpType.add).then_inc(S.vs, 1)
-            n += 1
-    g.sync.wait_ge(S.vs, n)
-    g.sync.dma_start(T.G[:], T.csb[:]).then_inc(S.st_g, 16)
-    g.wait_ge(S.st_g, 16)
-    off = [j for j in range(N) if topo.chip(keepers[j]) != topo.chip(core)]
-    on = [j for j in range(N) if topo.chip(keepers[j]) == topo.chip(core)]
-    tr = []
+    v.tensor_tensor(T.m75[:], T.msb[:], T.k75[:, 0:F], AluOpType.mult).then_inc(S.vs, 1)
+    v.tensor_tensor(T.tps[:, 0:F], T.msb[:], T.k75[:, F:2 * F], AluOpType.mult).then_inc(S.vs, 1)
+    v.wait_ge(S.vs, 4)
+    v.tensor_tensor(T.usb[:], T.wsb[:], T.tps[:, 0:F], AluOpType.add).then_inc(S.vs, 1)
+    others = [j for j in range(N) if j != rank]
+    others.sort(key=lambda j: 0 if topo.chip(cores[j]) != topo.chip(core) else 1)
+    eng = {}
     used = 0
-    for j in off:
-        e = _engines(topo.mask(core, keepers[j]) & ~used)[0]
+    for j in others:
+        e = _engines(topo.mask(core, cores[j]) & ~used)[0]
         used |= 1 << e
-        tr.append((j, e))
-    free = topo.mask(core, keepers[on[0]]) & ~used
-    for j, e in zip(on, _spread(_engines(free), len(on))):
-        tr.append((j, e))
+        eng[j] = e
+    g.wait_ge(S.ld_g, 16)
     g.remote_dma_fused(
-        [RemoteDMATransfer(dst_ids=[_dst(topo, keepers[j])], dma_engine_mask=1 << e, remote_sem=S.garr,
-                           src=_piece(T.G, j), dst=_piece(T.Lnd, rank)) for j, e in tr],
+        [RemoteDMATransfer(dst_ids=[_dst(topo, cores[j])], dma_engine_mask=1 << eng[j], remote_sem=S["a%d" % rank],
+                           src=T.gsb[:, F * j:F * j + F], dst=T.land[:, own]) for j in others],
         local_sem=S.ls)
-    total = 0
-    for k in keepers:
-        _o, _n, m_off, m_on = _keeper_masks(k, cores, topo)
-        total += len(_engines(m_on if topo.chip(k) == topo.chip(core) else m_off))
-    g.scalar.wait_ge(S.yarr, total)
-    g.scalar.dma_start(T.ysb[:], T.Y[rank::N, :]).then_inc(S.ldy, 16)
-    g.sync.wait_ge(S.yarr, total)
-    g.sync.dma_start(T.y[:], T.Y[:]).then_inc(S.fin, 16)
-    v.wait_ge(S.ldy, 16)
-    v.tensor_tensor(T.dsb[:], T.wsb[:], T.ysb[:], AluOpType.subtract).then_inc(S.vt, 1)
-    v.wait_ge(S.vt, 1)
-    v.tensor_tensor(T.mosb[:], T.dsb[:], T.dsb[:], AluOpType.add).then_inc(S.vt, 1)
-    g.scalar.wait_ge(S.vt, 2)
+    te.wait_ge(S.de, 32)
+    te.wait_ge(S.vs, 5)
+    te.matmul(T.Q[:, 0:F], T.eye[:], T.usb[:], True, False)
+    te.matmul(T.P[:, 0:F], T.eye[:], T.m75[:], True, False)
+    te.wait_ge(S.ld_g, 16)
+    te.matmul(T.Q[:, 0:F], T.hlf[:], T.gsb[:, own], False, False)
+    te.matmul(T.P[:, 0:F], T.eye[:], T.gsb[:, own], False, False)
+    order = sorted(others, key=lambda j: 0 if topo.chip(cores[j]) == topo.chip(core) else 1)
+    for i, s in enumerate(order):
+        last = i == len(order) - 1
+        te.wait_ge(S["a%d" % s], 1)
+        src = T.land[:, F * s:F * s + F]
+        q = te.matmul(T.Q[:, 0:F], T.hlf[:], src, False, last)
+        if last:
+            q.then_inc(S.qd, 1)
+        p = te.matmul(T.P[:, 0:F], T.eye[:], src, False, last)
+        if last:
+            p.then_inc(S.pd, 1)
+    v.wait_ge(S.qd, 1)
+    v.tensor_copy(T.ysb[:, own], T.Q[:, 0:F]).then_inc(S.wd, 1)
+    v.wait_ge(S.pd, 1)
+    v.tensor_copy(T.mosb[:], T.P[:, 0:F]).then_inc(S.md, 1)
+    g.wait_ge(S.wd, 1)
+    g.remote_dma_fused(
+        [RemoteDMATransfer(dst_ids=[_dst(topo, cores[j])], dma_engine_mask=1 << eng[j], remote_sem=S.yarr,
+                           src=T.ysb[:, own], dst=T.ysb[:, own]) for j in others],
+        local_sem=S.ls)
+    g.scalar.wait_ge(S.md, 1)
     g.scalar.dma_start(T.mo[:], T.mosb[:]).then_inc(S.fin, 16)
-    g.wait_ge(S.ls, len(tr))
+    g.sync.wait_ge(S.wd, 1)
+    g.sync.wait_ge(S.yarr, N - 1)
+    g.sync.dma_start(T.y[:], T.ysb[:]).then_inc(S.fin, 16)
+    g.wait_ge(S.ls, 2 * (N - 1))
     g.wait_ge(S.fin, 32)
-
-
-def rank_program(g, core, T, topo):
-    cores = list(T.cores)
-    keepers = _keepers(cores, topo)
-    rank = T.rank_of(core)
-    if rank is not None:
-        _rank(g, core, T, topo, cores, keepers, rank)
-    elif core in keepers:
-        _keeper(g, core, T, topo, cores, keepers.index(core))

@@ -11,30 +11,45 @@ SCRATCH = {
     "ysb": ("sbuf", [128, W], "bfloat16"),
     "msb": ("sbuf", [128, F], "bfloat16"),
     "wsb": ("sbuf", [128, F], "bfloat16"),
-    "m75": ("sbuf", [128, F], "bfloat16"),
-    "usb": ("sbuf", [128, F], "bfloat16"),
+    "w2": ("sbuf", [128, F], "float32"),
+    "xsb": ("sbuf", [128, F], "bfloat16"),
+    "dsb": ("sbuf", [128, F], "float32"),
     "mosb": ("sbuf", [128, F], "bfloat16"),
     "z1": ("sbuf", [128, F + 1], "bfloat16"),
-    "z2": ("sbuf", [128, F + 1], "bfloat16"),
-    "eye": ("sbuf", [128, F], "bfloat16"),
     "hlf": ("sbuf", [128, F], "bfloat16"),
-    "D": ("dram", [2, F + 1, F], "bfloat16"),
-    "k75": ("psum", [128, 512], "float32"),
+    "D": ("dram", [F + 1, F], "bfloat16"),
+    "kc": ("psum", [128, 512], "float32"),
     "tps": ("psum", [128, 512], "float32"),
-    "P": ("psum", [128, 512], "float32"),
     "Q": ("psum", [128, 512], "float32"),
 }
-SEMAPHORES = ["ld_g", "ld_mw", "vz", "vs", "dz", "de", "qd", "pd", "wd", "md", "yarr", "ls", "fin"] + \
-             ["a%d" % s for s in range(N)]
+SEMAPHORES = ["ld_a", "ld_b", "ld_mw", "vz", "vs", "dz", "de", "qd", "wd", "vd", "md", "ls", "fin"] + \
+             ["a%d" % s for s in range(N)] + ["y%d" % s for s in range(N)]
 
 
 def _engines(mask):
     return [e for e in range(mask.bit_length()) if (mask >> e) & 1]
 
 
+def _bits(engs):
+    m = 0
+    for e in engs:
+        m |= 1 << e
+    return m
+
+
 def _dst(topo, c):
     rid, pid, _se = topo.addr(c)
     return DstId(rid=rid, pnc=pid)
+
+
+def _runs(blocks):
+    out = []
+    for j in sorted(blocks):
+        if out and out[-1][1] == F * j:
+            out[-1][1] = F * j + F
+        else:
+            out.append([F * j, F * j + F])
+    return out
 
 
 def rank_program(g, core, T, topo):
@@ -46,72 +61,113 @@ def rank_program(g, core, T, topo):
     v = g.vector
     te = g.tensor
     own = slice(F * rank, F * rank + F)
-    g.sync.dma_start(T.gsb[:], T.gr[:]).then_inc(S.ld_g, 16)
+    chips = []
+    for c in cores:
+        if topo.chip(c) not in chips:
+            chips.append(topo.chip(c))
+    nc = len(chips)
+    me = chips.index(topo.chip(core))
+    half = (nc - 1) // 2
+
+    def on_chip(step):
+        return [j for j in range(N) if topo.chip(cores[j]) == chips[(me + step) % nc]]
+
+    peers = [j for j in on_chip(0) if j != rank]
+    near = [j for k in range(1, half + 1) for j in on_chip(k)]
+    far = [j for k in range(half + 1, nc) for j in on_chip(k)]
+    away = near + far
+    out_mask = topo.mask(core, cores[away[0]])
+    for j in away:
+        out_mask &= topo.mask(core, cores[j])
+    oe = _engines(out_mask)
+    ie = _engines(topo.mask(core, cores[peers[0]]) & ~out_mask)
+    eng = {}
+    for grp in (near, far):
+        k = len(oe) // len(grp)
+        for i, j in enumerate(grp):
+            eng[j] = oe[k * i:k * i + k]
+    for i, j in enumerate(peers):
+        eng[j] = ie[2 * i:2 * i + 2]
+    n_peer = len(eng[peers[0]])
+    n_away = len(eng[near[0]])
+
+    ra = _runs(near)
+    rb = _runs(far + peers + [rank])
+    for a, b in ra:
+        g.sync.dma_start(T.gsb[:, a:b], T.gr[:, a:b]).then_inc(S.ld_a, 16)
+    for a, b in rb:
+        g.sync.dma_start(T.gsb[:, a:b], T.gr[:, a:b]).then_inc(S.ld_b, 16)
+    v.memset(T.z1[:], 0.0).then_inc(S.vz, 1)
+    v.wait_ge(S.vz, 1)
+    v.memset(T.z1[:, 0:1], -0.5).then_inc(S.vz, 1)
+    g.scalar.wait_ge(S.vz, 2)
+    g.scalar.dma_start(T.D[:], T.z1[:]).then_inc(S.dz, 16)
     g.scalar.dma_start(T.msb[:], T.m[:]).then_inc(S.ld_mw, 16)
     g.scalar.dma_start(T.wsb[:], T.w[:]).then_inc(S.ld_mw, 16)
-    v.memset(T.z1[:], 0.0).then_inc(S.vz, 1)
-    v.memset(T.z2[:], 0.0).then_inc(S.vz, 1)
-    v.wait_ge(S.vz, 2)
-    v.memset(T.z1[:, 0:1], 1.0).then_inc(S.vz, 1)
-    v.memset(T.z2[:, 0:1], -0.5).then_inc(S.vz, 1)
-    g.scalar.wait_ge(S.vz, 4)
-    g.scalar.dma_start(T.D[0], T.z1[:]).then_inc(S.dz, 16)
-    g.scalar.dma_start(T.D[1], T.z2[:]).then_inc(S.dz, 16)
-    g.scalar.wait_ge(S.dz, 32)
-    g.scalar.dma_start(T.eye[:], T.D[0, 0:F, :]).then_inc(S.de, 16)
-    g.scalar.dma_start(T.hlf[:], T.D[1, 0:F, :]).then_inc(S.de, 16)
-    v.memset(T.k75[:, 0:F], 0.75).then_inc(S.vs, 1)
-    v.memset(T.k75[:, F:2 * F], -0.375).then_inc(S.vs, 1)
-    v.wait_ge(S.vs, 2)
+    g.scalar.wait_ge(S.dz, 16)
+    g.scalar.dma_start(T.hlf[:], T.D[0:F, :]).then_inc(S.de, 16)
+    v.memset(T.kc[:, 0:F], 0.75).then_inc(S.vs, 1)
+    v.wait_ge(S.vs, 1)
     v.wait_ge(S.ld_mw, 32)
-    v.tensor_tensor(T.m75[:], T.msb[:], T.k75[:, 0:F], AluOpType.mult).then_inc(S.vs, 1)
-    v.tensor_tensor(T.tps[:, 0:F], T.msb[:], T.k75[:, F:2 * F], AluOpType.mult).then_inc(S.vs, 1)
-    v.wait_ge(S.vs, 4)
-    v.tensor_tensor(T.usb[:], T.wsb[:], T.tps[:, 0:F], AluOpType.add).then_inc(S.vs, 1)
-    others = [j for j in range(N) if j != rank]
-    others.sort(key=lambda j: 0 if topo.chip(cores[j]) != topo.chip(core) else 1)
-    eng = {}
-    used = 0
-    for j in others:
-        e = _engines(topo.mask(core, cores[j]) & ~used)[0]
-        used |= 1 << e
-        eng[j] = e
-    g.wait_ge(S.ld_g, 16)
-    g.remote_dma_fused(
-        [RemoteDMATransfer(dst_ids=[_dst(topo, cores[j])], dma_engine_mask=1 << eng[j], remote_sem=S["a%d" % rank],
-                           src=T.gsb[:, F * j:F * j + F], dst=T.land[:, own]) for j in others],
-        local_sem=S.ls)
-    te.wait_ge(S.de, 32)
-    te.wait_ge(S.vs, 5)
-    te.matmul(T.Q[:, 0:F], T.eye[:], T.usb[:], True, False)
-    te.matmul(T.P[:, 0:F], T.eye[:], T.m75[:], True, False)
-    te.wait_ge(S.ld_g, 16)
+    v.tensor_tensor(T.tps[:, 0:F], T.msb[:], T.kc[:, 0:F], AluOpType.mult).then_inc(S.vs, 1)
+    v.tensor_tensor(T.w2[:], T.wsb[:], T.wsb[:], AluOpType.add).then_inc(S.vs, 1)
+    v.wait_ge(S.vs, 3)
+    v.tensor_tensor(T.xsb[:], T.tps[:, 0:F], T.w2[:], AluOpType.subtract).then_inc(S.vs, 1)
+
+    def scatter(js):
+        g.remote_dma_fused(
+            [RemoteDMATransfer(dst_ids=[_dst(topo, cores[j])], dma_engine_mask=_bits(eng[j]),
+                               remote_sem=S["a%d" % rank], src=T.gsb[:, F * j:F * j + F], dst=T.land[:, own])
+             for j in js], local_sem=S.ls)
+
+    g.wait_ge(S.ld_a, 16 * len(ra))
+    scatter(near)
+    g.wait_ge(S.ld_b, 16 * len(rb))
+    scatter(far + peers)
+    te.wait_ge(S.de, 16)
+    te.wait_ge(S.vs, 4)
+    te.matmul(T.Q[:, 0:F], T.hlf[:], T.xsb[:], True, False)
+    te.wait_ge(S.ld_b, 16 * len(rb))
     te.matmul(T.Q[:, 0:F], T.hlf[:], T.gsb[:, own], False, False)
-    te.matmul(T.P[:, 0:F], T.eye[:], T.gsb[:, own], False, False)
-    order = sorted(others, key=lambda j: 0 if topo.chip(cores[j]) == topo.chip(core) else 1)
+    early = [j for k in range(1, half + 1) for j in on_chip(-k)]
+    late = [j for k in range(half + 1, nc) for j in on_chip(-k)]
+    order = early + peers + late
     for i, s in enumerate(order):
         last = i == len(order) - 1
-        te.wait_ge(S["a%d" % s], 1)
-        src = T.land[:, F * s:F * s + F]
-        q = te.matmul(T.Q[:, 0:F], T.hlf[:], src, False, last)
+        te.wait_ge(S["a%d" % s], n_peer if s in peers else n_away)
+        q = te.matmul(T.Q[:, 0:F], T.hlf[:], T.land[:, F * s:F * s + F], False, last)
         if last:
             q.then_inc(S.qd, 1)
-        p = te.matmul(T.P[:, 0:F], T.eye[:], src, False, last)
-        if last:
-            p.then_inc(S.pd, 1)
     v.wait_ge(S.qd, 1)
     v.tensor_copy(T.ysb[:, own], T.Q[:, 0:F]).then_inc(S.wd, 1)
-    v.wait_ge(S.pd, 1)
-    v.tensor_copy(T.mosb[:], T.P[:, 0:F]).then_inc(S.md, 1)
+    v.tensor_tensor(T.dsb[:], T.wsb[:], T.Q[:, 0:F], AluOpType.subtract).then_inc(S.vd, 1)
+    v.wait_ge(S.vd, 1)
+    v.tensor_tensor(T.mosb[:], T.dsb[:], T.dsb[:], AluOpType.add).then_inc(S.md, 1)
+
     g.wait_ge(S.wd, 1)
     g.remote_dma_fused(
-        [RemoteDMATransfer(dst_ids=[_dst(topo, cores[j])], dma_engine_mask=1 << eng[j], remote_sem=S.yarr,
-                           src=T.ysb[:, own], dst=T.ysb[:, own]) for j in others],
+        [RemoteDMATransfer(dst_ids=[_dst(topo, cores[j]) for j in away], dma_engine_mask=out_mask,
+                           remote_sem=S["y%d" % rank], srcs=[T.ysb[:, own]], dsts=[T.ysb[:, own] for _ in away]),
+         RemoteDMATransfer(dst_ids=[_dst(topo, cores[j]) for j in peers], dma_engine_mask=_bits(eng[peers[0]]),
+                           remote_sem=S["y%d" % rank], srcs=[T.ysb[:, own]], dsts=[T.ysb[:, own] for _ in peers])],
         local_sem=S.ls)
+
+    def store(q, srcs, extra):
+        for s in srcs:
+            q.wait_ge(S["y%d" % s], n_peer if s in peers else len(oe))
+        n = 0
+        for a, b in _runs(srcs + extra):
+            q.dma_start(T.y[:, a:b], T.ysb[:, a:b]).then_inc(S.fin, 16)
+            n += 1
+        return n
+
     g.scalar.wait_ge(S.md, 1)
     g.scalar.dma_start(T.mo[:], T.mosb[:]).then_inc(S.fin, 16)
-    g.sync.wait_ge(S.wd, 1)
-    g.sync.wait_ge(S.yarr, N - 1)
-    g.sync.dma_start(T.y[:], T.ysb[:]).then_inc(S.fin, 16)
-    g.wait_ge(S.ls, 2 * (N - 1))
-    g.wait_ge(S.fin, 32)
+    nfin = 1
+    g.scalar.wait_ge(S.wd, 1)
+    first = [j for k in range(1, nc - 2) for j in on_chip(-k)]
+    nfin += store(g.scalar, peers + first, [rank])
+    nfin += store(g.scalar, on_chip(2 - nc), [])
+    nfin += store(g.sync, on_chip(1 - nc), [])
+    g.wait_ge(S.ls, n_away * len(away) + n_peer + len(oe) + n_peer)
+    g.wait_ge(S.fin, 16 * nfin)

@@ -11,18 +11,13 @@ SCRATCH = {
     "ysb": ("sbuf", [128, W], "bfloat16"),
     "msb": ("sbuf", [128, F], "bfloat16"),
     "wsb": ("sbuf", [128, F], "bfloat16"),
-    "w2": ("sbuf", [128, F], "float32"),
-    "xsb": ("sbuf", [128, F], "bfloat16"),
-    "dsb": ("sbuf", [128, F], "float32"),
     "mosb": ("sbuf", [128, F], "bfloat16"),
-    "z1": ("sbuf", [128, F + 1], "bfloat16"),
+    "cst": ("sbuf", [128, F], "bfloat16"),
     "hlf": ("sbuf", [128, F], "bfloat16"),
-    "D": ("dram", [F + 1, F], "bfloat16"),
-    "kc": ("psum", [128, 512], "float32"),
-    "tps": ("psum", [128, 512], "float32"),
+    "h2": ("sbuf", [128, F], "bfloat16"),
     "Q": ("psum", [128, 512], "float32"),
 }
-SEMAPHORES = ["ld_a", "ld_b", "ld_mw", "vz", "vs", "dz", "de", "qd", "wd", "vd", "md", "ls", "fin"] + \
+SEMAPHORES = ["ld_a", "ld_b", "ld_c", "ld_mw", "vz", "vs", "de", "qd", "wd", "md", "ls", "fin"] + \
              ["a%d" % s for s in range(N)] + ["y%d" % s for s in range(N)]
 
 
@@ -52,6 +47,10 @@ def _runs(blocks):
     return out
 
 
+def _blk(j):
+    return slice(F * j, F * j + F)
+
+
 def rank_program(g, core, T, topo):
     rank = T.rank_of(core)
     if rank is None:
@@ -60,7 +59,7 @@ def rank_program(g, core, T, topo):
     S = T.sem
     v = g.vector
     te = g.tensor
-    own = slice(F * rank, F * rank + F)
+    own = _blk(rank)
     chips = []
     for c in cores:
         if topo.chip(c) not in chips:
@@ -72,102 +71,114 @@ def rank_program(g, core, T, topo):
     def on_chip(step):
         return [j for j in range(N) if topo.chip(cores[j]) == chips[(me + step) % nc]]
 
-    peers = [j for j in on_chip(0) if j != rank]
-    near = [j for k in range(1, half + 1) for j in on_chip(k)]
-    far = [j for k in range(half + 1, nc) for j in on_chip(k)]
-    away = near + far
-    out_mask = topo.mask(core, cores[away[0]])
-    for j in away:
+    def sd(step):
+        return [j for j in on_chip(step) if topo.die(cores[j]) == topo.die(core)][0]
+
+    def od(step):
+        return [j for j in on_chip(step) if topo.die(cores[j]) != topo.die(core)][0]
+
+    peer = od(0)
+    others = [j for k in range(1, nc) for j in on_chip(k)]
+    out_mask = topo.mask(core, cores[others[0]])
+    for j in others:
         out_mask &= topo.mask(core, cores[j])
     oe = _engines(out_mask)
-    ie = _engines(topo.mask(core, cores[peers[0]]) & ~out_mask)
-    eng = {}
-    for grp in (near, far):
-        k = len(oe) // len(grp)
-        for i, j in enumerate(grp):
-            eng[j] = oe[k * i:k * i + k]
-    for i, j in enumerate(peers):
-        eng[j] = ie[2 * i:2 * i + 2]
-    n_peer = len(eng[peers[0]])
-    n_away = len(eng[near[0]])
+    ie = _engines(topo.mask(core, cores[peer]) & ~out_mask)
+    sent = [0]
 
-    ra = _runs(near)
-    rb = _runs(far + peers + [rank])
-    for a, b in ra:
-        g.sync.dma_start(T.gsb[:, a:b], T.gr[:, a:b]).then_inc(S.ld_a, 16)
-    for a, b in rb:
-        g.sync.dma_start(T.gsb[:, a:b], T.gr[:, a:b]).then_inc(S.ld_b, 16)
-    v.memset(T.z1[:], 0.0).then_inc(S.vz, 1)
-    v.wait_ge(S.vz, 1)
-    v.memset(T.z1[:, 0:1], -0.5).then_inc(S.vz, 1)
-    g.scalar.wait_ge(S.vz, 2)
-    g.scalar.dma_start(T.D[:], T.z1[:]).then_inc(S.dz, 16)
-    g.scalar.dma_start(T.msb[:], T.m[:]).then_inc(S.ld_mw, 16)
-    g.scalar.dma_start(T.wsb[:], T.w[:]).then_inc(S.ld_mw, 16)
-    g.scalar.wait_ge(S.dz, 16)
-    g.scalar.dma_start(T.hlf[:], T.D[0:F, :]).then_inc(S.de, 16)
-    v.memset(T.kc[:, 0:F], 0.75).then_inc(S.vs, 1)
-    v.wait_ge(S.vs, 1)
-    v.wait_ge(S.ld_mw, 32)
-    v.tensor_tensor(T.tps[:, 0:F], T.msb[:], T.kc[:, 0:F], AluOpType.mult).then_inc(S.vs, 1)
-    v.tensor_tensor(T.w2[:], T.wsb[:], T.wsb[:], AluOpType.add).then_inc(S.vs, 1)
-    v.wait_ge(S.vs, 3)
-    v.tensor_tensor(T.xsb[:], T.tps[:, 0:F], T.w2[:], AluOpType.subtract).then_inc(S.vs, 1)
+    def call(transfers, n):
+        g.remote_dma_fused(transfers, local_sem=S.ls)
+        sent[0] += n
+
+    waves = [[1], list(range(2, nc - 1)), [nc - 1]]
+
+    def wave(i, sign):
+        return [j for k in waves[i] for j in on_chip(sign * k)]
+
+    parts = [_runs(wave(0, 1)), _runs(wave(1, 1) + [rank, peer]), _runs(wave(2, 1))]
+    lds = [S.ld_a, S.ld_b, S.ld_c]
+    for rs, ld in zip(parts, lds):
+        for a, b in rs:
+            g.sync.dma_start(T.gsb[:, a:b], T.gr[:, a:b]).then_inc(ld, 16)
+    g.sync.dma_start(T.msb[:], T.m[:]).then_inc(S.ld_mw, 16)
+    g.sync.dma_start(T.wsb[:], T.w[:]).then_inc(S.ld_mw, 16)
+    v.memset(T.cst[:], -0.5).then_inc(S.vz, 1)
+    g.wait_ge(S.vz, 1)
+    g.affine_select(T.hlf[:], T.cst[:], [[-1, F]], AluOpType.is_equal, 0.0, 0, 1).then_inc(S.de, 1)
+    v.wait_ge(S.de, 1)
+    v.tensor_scalar(T.h2[:], T.hlf[:], 0.75, None, AluOpType.mult).then_inc(S.vs, 1)
 
     def scatter(js):
-        g.remote_dma_fused(
-            [RemoteDMATransfer(dst_ids=[_dst(topo, cores[j])], dma_engine_mask=_bits(eng[j]),
-                               remote_sem=S["a%d" % rank], src=T.gsb[:, F * j:F * j + F], dst=T.land[:, own])
-             for j in js], local_sem=S.ls)
+        n = len(oe) // len(js)
+        return [RemoteDMATransfer(dst_ids=[_dst(topo, cores[j])], dma_engine_mask=_bits(oe[n * i:n * i + n]),
+                                  remote_sem=S["a%d" % rank], src=T.gsb[:, _blk(j)], dst=T.land[:, own])
+                for i, j in enumerate(js)]
 
-    g.wait_ge(S.ld_a, 16 * len(ra))
-    scatter(near)
-    g.wait_ge(S.ld_b, 16 * len(rb))
-    scatter(far + peers)
-    te.wait_ge(S.de, 16)
-    te.wait_ge(S.vs, 4)
-    te.matmul(T.Q[:, 0:F], T.hlf[:], T.xsb[:], True, False)
-    te.wait_ge(S.ld_b, 16 * len(rb))
-    te.matmul(T.Q[:, 0:F], T.hlf[:], T.gsb[:, own], False, False)
-    early = [j for k in range(1, half + 1) for j in on_chip(-k)]
-    late = [j for k in range(half + 1, nc) for j in on_chip(-k)]
-    order = early + peers + late
-    for i, s in enumerate(order):
+    g.wait_ge(S.ld_a, 16 * len(parts[0]))
+    call(scatter(wave(0, 1)), len(oe))
+    g.wait_ge(S.ld_b, 16 * len(parts[1]))
+    call(scatter(wave(1, 1)) +
+         [RemoteDMATransfer(dst_ids=[_dst(topo, cores[peer])], dma_engine_mask=_bits(ie),
+                            remote_sem=S["a%d" % rank], src=T.gsb[:, _blk(peer)], dst=T.land[:, own])], len(oe) + len(ie))
+    g.wait_ge(S.ld_c, 16 * len(parts[2]))
+    call(scatter(wave(2, 1)), len(oe))
+
+    te.wait_ge(S.de, 1)
+    te.wait_ge(S.ld_b, 16 * len(parts[1]))
+    te.matmul(T.Q[:, 0:F], T.hlf[:], T.gsb[:, own], True, False)
+    te.wait_ge(S.vs, 1)
+    te.wait_ge(S.ld_mw, 32)
+    te.matmul(T.Q[:, 0:F], T.h2[:], T.msb[:], False, False)
+    order = [(j, len(oe) // len(wave(0, -1))) for j in wave(0, -1)] + [(peer, len(ie))] + \
+            [(j, len(oe) // len(wave(1, -1))) for j in wave(1, -1)] + \
+            [(j, len(oe) // len(wave(2, -1))) for j in wave(2, -1)]
+    for i, (s, n) in enumerate(order):
         last = i == len(order) - 1
-        te.wait_ge(S["a%d" % s], n_peer if s in peers else n_away)
-        q = te.matmul(T.Q[:, 0:F], T.hlf[:], T.land[:, F * s:F * s + F], False, last)
+        te.wait_ge(S["a%d" % s], n)
+        q = te.matmul(T.Q[:, 0:F], T.hlf[:], T.land[:, _blk(s)], False, last)
         if last:
             q.then_inc(S.qd, 1)
+    v.wait_ge(S.ld_mw, 32)
     v.wait_ge(S.qd, 1)
-    v.tensor_copy(T.ysb[:, own], T.Q[:, 0:F]).then_inc(S.wd, 1)
-    v.tensor_tensor(T.dsb[:], T.wsb[:], T.Q[:, 0:F], AluOpType.subtract).then_inc(S.vd, 1)
-    v.wait_ge(S.vd, 1)
-    v.tensor_tensor(T.mosb[:], T.dsb[:], T.dsb[:], AluOpType.add).then_inc(S.md, 1)
+    v.tensor_tensor(T.ysb[:, own], T.Q[:, 0:F], T.wsb[:], AluOpType.add).then_inc(S.wd, 1)
+    v.tensor_scalar(T.mosb[:], T.Q[:, 0:F], -2.0, None, AluOpType.mult).then_inc(S.md, 1)
 
+    one_steps = list(range(1, half + 1))
+    two_steps = list(range(half + 1, nc))
+    away = [sd(k) for k in one_steps] + [j for k in two_steps for j in (sd(k), od(k))]
     g.wait_ge(S.wd, 1)
-    g.remote_dma_fused(
-        [RemoteDMATransfer(dst_ids=[_dst(topo, cores[j]) for j in away], dma_engine_mask=out_mask,
-                           remote_sem=S["y%d" % rank], srcs=[T.ysb[:, own]], dsts=[T.ysb[:, own] for _ in away]),
-         RemoteDMATransfer(dst_ids=[_dst(topo, cores[j]) for j in peers], dma_engine_mask=_bits(eng[peers[0]]),
-                           remote_sem=S["y%d" % rank], srcs=[T.ysb[:, own]], dsts=[T.ysb[:, own] for _ in peers])],
-        local_sem=S.ls)
+    call([RemoteDMATransfer(dst_ids=[_dst(topo, cores[j]) for j in away], dma_engine_mask=out_mask,
+                            remote_sem=S["y%d" % rank], srcs=[T.ysb[:, own]], dsts=[T.ysb[:, own] for _ in away]),
+          RemoteDMATransfer(dst_ids=[_dst(topo, cores[peer])], dma_engine_mask=_bits(ie),
+                            remote_sem=S["y%d" % rank], srcs=[T.ysb[:, own]], dsts=[T.ysb[:, own]])], len(oe) + len(ie))
+    for k in one_steps:
+        s = sd(-k)
+        g.wait_ge(S["y%d" % s], len(oe))
+        call([RemoteDMATransfer(dst_ids=[_dst(topo, cores[peer])], dma_engine_mask=_bits(ie),
+                                remote_sem=S["y%d" % s], src=T.ysb[:, _blk(s)], dst=T.ysb[:, _blk(s)])], len(ie))
+
+    def n_y(s):
+        if s == peer or s in [od(-k) for k in one_steps]:
+            return len(ie)
+        return len(oe)
 
     def store(q, srcs, extra):
         for s in srcs:
-            q.wait_ge(S["y%d" % s], n_peer if s in peers else len(oe))
+            q.wait_ge(S["y%d" % s], n_y(s))
         n = 0
         for a, b in _runs(srcs + extra):
             q.dma_start(T.y[:, a:b], T.ysb[:, a:b]).then_inc(S.fin, 16)
             n += 1
         return n
 
-    g.scalar.wait_ge(S.md, 1)
-    g.scalar.dma_start(T.mo[:], T.mosb[:]).then_inc(S.fin, 16)
     nfin = 1
+    g.sync.wait_ge(S.md, 1)
+    g.sync.dma_start(T.mo[:], T.mosb[:]).then_inc(S.fin, 16)
     g.scalar.wait_ge(S.wd, 1)
-    first = [j for k in range(1, nc - 2) for j in on_chip(-k)]
-    nfin += store(g.scalar, peers + first, [rank])
-    nfin += store(g.scalar, on_chip(2 - nc), [])
-    nfin += store(g.sync, on_chip(1 - nc), [])
-    g.wait_ge(S.ls, n_away * len(away) + n_peer + len(oe) + n_peer)
+    nfin += store(g.scalar, [peer] + on_chip(-one_steps[0]), [rank])
+    for k in one_steps[1:]:
+        nfin += store(g.scalar, on_chip(-k), [])
+    for k in two_steps:
+        nfin += store(g.sync, on_chip(-k), [])
+    g.wait_ge(S.ls, sent[0])
     g.wait_ge(S.fin, 16 * nfin)

from concourse.bass import DstId, RemoteDMATransfer
from concourse.mybir import AluOpType

N = 10
F = 128
W = N * F

SCRATCH = {
    "gsb": ("sbuf", [128, W], "bfloat16"),
    "land": ("sbuf", [128, W], "bfloat16"),
    "ysb": ("sbuf", [128, W], "bfloat16"),
    "msb": ("sbuf", [128, F], "bfloat16"),
    "wsb": ("sbuf", [128, F], "bfloat16"),
    "mosb": ("sbuf", [128, F], "bfloat16"),
    "cst": ("sbuf", [128, F], "bfloat16"),
    "hlf": ("sbuf", [128, F], "bfloat16"),
    "h2": ("sbuf", [128, F], "bfloat16"),
    "Q": ("psum", [128, 512], "float32"),
}
SEMAPHORES = ["ld_a", "ld_b", "ld_c", "ld_mw", "vz", "vs", "de", "qd", "wd", "md", "ls", "fin"] + \
             ["a%d" % s for s in range(N)] + ["y%d" % s for s in range(N)]


def _engines(mask):
    return [e for e in range(mask.bit_length()) if (mask >> e) & 1]


def _bits(engs):
    m = 0
    for e in engs:
        m |= 1 << e
    return m


def _dst(topo, c):
    rid, pid, _se = topo.addr(c)
    return DstId(rid=rid, pnc=pid)


def _runs(blocks):
    out = []
    for j in sorted(blocks):
        if out and out[-1][1] == F * j:
            out[-1][1] = F * j + F
        else:
            out.append([F * j, F * j + F])
    return out


def _blk(j):
    return slice(F * j, F * j + F)


def rank_program(g, core, T, topo):
    rank = T.rank_of(core)
    if rank is None:
        return
    cores = list(T.cores)
    S = T.sem
    v = g.vector
    te = g.tensor
    own = _blk(rank)
    chips = []
    for c in cores:
        if topo.chip(c) not in chips:
            chips.append(topo.chip(c))
    nc = len(chips)
    me = chips.index(topo.chip(core))
    half = (nc - 1) // 2

    def on_chip(step):
        return [j for j in range(N) if topo.chip(cores[j]) == chips[(me + step) % nc]]

    def sd(step):
        return [j for j in on_chip(step) if topo.die(cores[j]) == topo.die(core)][0]

    def od(step):
        return [j for j in on_chip(step) if topo.die(cores[j]) != topo.die(core)][0]

    peer = od(0)
    others = [j for k in range(1, nc) for j in on_chip(k)]
    out_mask = topo.mask(core, cores[others[0]])
    for j in others:
        out_mask &= topo.mask(core, cores[j])
    oe = _engines(out_mask)
    ie = _engines(topo.mask(core, cores[peer]) & ~out_mask)
    sent = [0]

    def call(transfers, n):
        g.remote_dma_fused(transfers, local_sem=S.ls)
        sent[0] += n

    waves = [[1], list(range(2, nc - 1)), [nc - 1]]

    def wave(i, sign):
        return [j for k in waves[i] for j in on_chip(sign * k)]

    parts = [_runs(wave(0, 1)), _runs(wave(1, 1) + [rank, peer]), _runs(wave(2, 1))]
    lds = [S.ld_a, S.ld_b, S.ld_c]
    for rs, ld in zip(parts, lds):
        for a, b in rs:
            g.sync.dma_start(T.gsb[:, a:b], T.gr[:, a:b]).then_inc(ld, 16)
    g.sync.dma_start(T.msb[:], T.m[:]).then_inc(S.ld_mw, 16)
    g.sync.dma_start(T.wsb[:], T.w[:]).then_inc(S.ld_mw, 16)
    v.memset(T.cst[:], -0.5).then_inc(S.vz, 1)
    g.wait_ge(S.vz, 1)
    g.affine_select(T.hlf[:], T.cst[:], [[-1, F]], AluOpType.is_equal, 0.0, 0, 1).then_inc(S.de, 1)
    v.wait_ge(S.de, 1)
    v.tensor_scalar(T.h2[:], T.hlf[:], 0.75, None, AluOpType.mult).then_inc(S.vs, 1)

    def scatter(js):
        n = len(oe) // len(js)
        return [RemoteDMATransfer(dst_ids=[_dst(topo, cores[j])], dma_engine_mask=_bits(oe[n * i:n * i + n]),
                                  remote_sem=S["a%d" % rank], src=T.gsb[:, _blk(j)], dst=T.land[:, own])
                for i, j in enumerate(js)]

    g.wait_ge(S.ld_a, 16 * len(parts[0]))
    call(scatter(wave(0, 1)), len(oe))
    g.wait_ge(S.ld_b, 16 * len(parts[1]))
    call(scatter(wave(1, 1)) +
         [RemoteDMATransfer(dst_ids=[_dst(topo, cores[peer])], dma_engine_mask=_bits(ie),
                            remote_sem=S["a%d" % rank], src=T.gsb[:, _blk(peer)], dst=T.land[:, own])], len(oe) + len(ie))
    g.wait_ge(S.ld_c, 16 * len(parts[2]))
    call(scatter(wave(2, 1)), len(oe))

    te.wait_ge(S.de, 1)
    te.wait_ge(S.ld_b, 16 * len(parts[1]))
    te.matmul(T.Q[:, 0:F], T.hlf[:], T.gsb[:, own], True, False)
    te.wait_ge(S.vs, 1)
    te.wait_ge(S.ld_mw, 32)
    te.matmul(T.Q[:, 0:F], T.h2[:], T.msb[:], False, False)
    order = [(j, len(oe) // len(wave(0, -1))) for j in wave(0, -1)] + [(peer, len(ie))] + \
            [(j, len(oe) // len(wave(1, -1))) for j in wave(1, -1)] + \
            [(j, len(oe) // len(wave(2, -1))) for j in wave(2, -1)]
    for i, (s, n) in enumerate(order):
        last = i == len(order) - 1
        te.wait_ge(S["a%d" % s], n)
        q = te.matmul(T.Q[:, 0:F], T.hlf[:], T.land[:, _blk(s)], False, last)
        if last:
            q.then_inc(S.qd, 1)
    v.wait_ge(S.ld_mw, 32)
    v.wait_ge(S.qd, 1)
    v.tensor_tensor(T.ysb[:, own], T.Q[:, 0:F], T.wsb[:], AluOpType.add).then_inc(S.wd, 1)
    v.tensor_scalar(T.mosb[:], T.Q[:, 0:F], -2.0, None, AluOpType.mult).then_inc(S.md, 1)

    one_steps = list(range(1, half + 1))
    two_steps = list(range(half + 1, nc))
    away = [sd(k) for k in one_steps] + [j for k in two_steps for j in (sd(k), od(k))]
    g.wait_ge(S.wd, 1)
    call([RemoteDMATransfer(dst_ids=[_dst(topo, cores[j]) for j in away], dma_engine_mask=out_mask,
                            remote_sem=S["y%d" % rank], srcs=[T.ysb[:, own]], dsts=[T.ysb[:, own] for _ in away]),
          RemoteDMATransfer(dst_ids=[_dst(topo, cores[peer])], dma_engine_mask=_bits(ie),
                            remote_sem=S["y%d" % rank], srcs=[T.ysb[:, own]], dsts=[T.ysb[:, own]])], len(oe) + len(ie))
    for k in one_steps:
        s = sd(-k)
        g.wait_ge(S["y%d" % s], len(oe))
        call([RemoteDMATransfer(dst_ids=[_dst(topo, cores[peer])], dma_engine_mask=_bits(ie),
                                remote_sem=S["y%d" % s], src=T.ysb[:, _blk(s)], dst=T.ysb[:, _blk(s)])], len(ie))

    def n_y(s):
        if s == peer or s in [od(-k) for k in one_steps]:
            return len(ie)
        return len(oe)

    def store(q, srcs, extra):
        for s in srcs:
            q.wait_ge(S["y%d" % s], n_y(s))
        n = 0
        for a, b in _runs(srcs + extra):
            q.dma_start(T.y[:, a:b], T.ysb[:, a:b]).then_inc(S.fin, 16)
            n += 1
        return n

    nfin = 1
    g.sync.wait_ge(S.md, 1)
    g.sync.dma_start(T.mo[:], T.mosb[:]).then_inc(S.fin, 16)
    g.scalar.wait_ge(S.wd, 1)
    nfin += store(g.scalar, [peer] + on_chip(-one_steps[0]), [rank])
    for k in one_steps[1:]:
        nfin += store(g.scalar, on_chip(-k), [])
    for k in two_steps:
        nfin += store(g.sync, on_chip(-k), [])
    g.wait_ge(S.ls, sent[0])
    g.wait_ge(S.fin, 16 * nfin)
